import numpy as np
import ml_dtypes


def mxq(x, axis, fmt="e4m3"):
    dtype, down = {"e4m3": (ml_dtypes.float8_e4m3fn, 7), "e5m2": (ml_dtypes.float8_e5m2, 14)}[fmt]
    v = np.moveaxis(np.asarray(x, np.float32).astype(ml_dtypes.bfloat16).astype(np.float64), axis, -1)
    blocks = v.reshape(v.shape[:-1] + (-1, 32))
    amax = np.abs(blocks).max(-1, keepdims=True)
    byte = np.maximum(np.where(amax > 0, np.frexp(amax)[1] - 1 + 127, 0) - down, 1)
    scale = np.exp2(byte - 127.0)
    codes = (blocks / scale).astype(np.float32).astype(dtype).astype(np.float64)
    return np.moveaxis((codes * scale).reshape(v.shape), -1, axis)


WIDE = False


def mx_kscale(k):
    if not WIDE:
        return np.ones(k)
    levels = np.array([10, -10, 5, -5, 0])
    if k % 512:
        return np.exp2(np.random.permutation(np.resize(levels, k // 32))).repeat(32)
    a = np.empty((k // 512, 16))
    for p in range(k // 512):
        a[p, :8] = np.random.permutation(np.resize(levels, 8))
        for g in range(8):
            far = levels[np.abs(levels - a[p, g]) >= 10]
            a[p, g + 8] = far[np.random.randint(len(far))]
    return np.exp2(a.ravel()).repeat(32)


def f64(x):
    return np.asarray(x).astype(np.float64)


def striped(idx):
    return np.tile(idx.reshape(-1, 16).T, (8, 1)).astype(np.uint16)


def unstriped(offs):
    return offs[:16].T.reshape(-1).astype(np.int64)


def pack_weight(w):
    k, n = w.shape
    w = f64(np.asarray(w, np.float32).astype(ml_dtypes.bfloat16)).reshape(k // 32, 32, n)
    amax = np.abs(w).max(1)
    byte = np.clip(np.where(amax > 0, np.frexp(amax)[1] - 1 + 127 - 7, 1), 1, 254)
    scaled = (w * np.exp2(127.0 - byte)[:, None, :]).reshape(k, n).astype(np.float32)
    words = np.ascontiguousarray(scaled.reshape(k // 512, 128, 4, n).transpose(0, 1, 3, 2)).astype(ml_dtypes.float8_e4m3fn).view(np.uint8)
    return words, np.ascontiguousarray(byte.astype(np.uint8).reshape(k // 512, 16, n))


def unpack_weight(words, scales):
    g, p, n, _ = words.shape
    vals = np.ascontiguousarray(words).view(ml_dtypes.float8_e4m3fn).astype(np.float64) * np.repeat(np.exp2(scales.astype(np.float64) - 127.0), 8, axis=1)[..., None]
    return vals.transpose(0, 1, 3, 2).reshape(g * 512, n)


E2M1 = np.array([0.0, 0.5, 1.0, 1.5, 2.0, 3.0, 4.0, 6.0, -0.0, -0.5, -1.0, -1.5, -2.0, -3.0, -4.0, -6.0])


def pack_fp4(w):
    k, n = w.shape
    w = f64(np.asarray(w, np.float32).astype(ml_dtypes.bfloat16)).reshape(k // 32, 32, n)
    amax = np.abs(w).max(1)
    mant, ex = np.frexp(amax / 6.0)
    byte = np.clip(np.where(amax > 0, np.where(mant > 0.5, ex, ex - 1) + 127, 1), 1, 254)
    scaled = (w * np.exp2(127.0 - byte)[:, None, :]).reshape(k, n).astype(np.float32)
    c = np.ascontiguousarray(scaled.reshape(k // 512, 128, 4, n).transpose(0, 1, 3, 2)).astype(ml_dtypes.float4_e2m1fn).view(np.uint8) & 0xF
    words = (c[..., 0::2] | (c[..., 1::2] << 4)).reshape(k // 512, 128, 2 * n)
    return np.ascontiguousarray(words), np.ascontiguousarray(byte.astype(np.uint8).reshape(k // 512, 16, n))


def unpack_fp4(words, scales):
    g, _, n = scales.shape
    words = np.ascontiguousarray(words).reshape(g, 128, n, 2)
    nib = np.empty((g, 128, n, 4), np.uint8)
    nib[..., 0::2] = words & 0xF
    nib[..., 1::2] = words >> 4
    vals = E2M1[nib] * np.repeat(np.exp2(scales.astype(np.float64) - 127.0), 8, axis=1)[..., None]
    return vals.transpose(0, 1, 3, 2).reshape(g * 512, n)


def relu(v):
    return np.maximum(v, 0.0)


K, T, S, N, H, U = 512, 2048, 512, 128, 512, 1024


def setup_inputs():
    n = np.random.standard_normal
    s = mx_kscale(K)[:, None]
    u = mx_kscale(H)
    packed_xT = pack_weight(n((K, T)) * s)
    packed_w1 = pack_fp4(n((K, H)) / np.sqrt(K) / s)
    packed_w2 = pack_fp4(n((K, H)) / np.sqrt(K) / s)
    packed_w3 = pack_fp4(n((H, N)) / np.sqrt(H) / u[:, None])
    return {
        "x_words": packed_xT[0],
        "x_scales": packed_xT[1],
        "w1_words": packed_w1[0],
        "w1_scales": packed_w1[1],
        "w2_words": packed_w2[0],
        "w2_scales": packed_w2[1],
        "unit": (np.random.uniform(0.6, 1.4, (H, 1)) * u[:, None]).astype(np.float32),
        "w3_words": packed_w3[0],
        "w3_scales": packed_w3[1],
        "offs": striped(np.random.permutation(T)[:S]),
        "me": striped(np.random.permutation(np.concatenate([np.arange(S), np.random.randint(0, S, U - S)]))),
        "ot": striped(np.random.permutation(np.concatenate([np.arange(S), np.random.randint(0, S, U - S)]))),
    }


def reference(x_words, x_scales, w1_words, w1_scales, w2_words, w2_scales, unit, w3_words, w3_scales, offs, me, ot):
    xq = unpack_weight(x_words, x_scales)[:, unstriped(offs)]
    px = unpack_fp4(w1_words, w1_scales).T @ xq
    xo = px[:, unstriped(ot)]
    xm = px[:, unstriped(me)]
    dx = xo - xm
    vx = unpack_fp4(w2_words, w2_scales).T @ xq
    vm = vx[:, unstriped(me)]
    vo = vx[:, unstriped(ot)]
    dv = vm - vo
    cls = dx * dv
    ttc = (relu(cls) + 0.1) / ((dv) ** 2 + 0.3)
    ener = np.exp(-1.0 * ttc) / ((ttc) ** 2 + 0.3)
    hid = f64(unit) * (np.log(ener) - (0.4 * dv))
    return unpack_fp4(w3_words, w3_scales).T @ mxq(hid, 0, "e4m3")

@@ -1,0 +1,186 @@
+from contextlib import ExitStack
+
+import concourse.mybir as mybir
+from concourse.masks import make_identity
+
+K, T, S, N, H, U = 512, 2048, 512, 128, 512, 1024
+FLOPS = 2 * K * H * S * 2 + 2 * H * N * U
+
+F32 = mybir.dt.float32
+BF16 = mybir.dt.bfloat16
+I32 = mybir.dt.int32
+U32 = mybir.dt.uint32
+U16 = mybir.dt.uint16
+U8 = mybir.dt.uint8
+FP8X4 = mybir.dt.float8_e4m3fn_x4
+FP4X4 = mybir.dt.float4_e2m1fn_x4
+ACT = mybir.ActivationFunctionType
+ALU = mybir.AluOpType
+
+P = 128
+PACK = 4
+BLOCKS = H // P
+CHUNK = 128
+CHUNKS = U // CHUNK
+SPAN = 256
+SPANS = U // SPAN
+BANKS = 8
+
+
+def tile_picked_yttcpl_log_p_kernel(
+    tc, x_words, x_scales, w1_words, w1_scales, w2_words, w2_scales, unit, w3_words, w3_scales, offs, me, ot, out
+):
+    nc = tc.nc
+    with ExitStack() as ctx:
+        keep = ctx.enter_context(tc.tile_pool(name="keep", bufs=1))
+        ring = ctx.enter_context(tc.tile_pool(name="ring", bufs=2))
+        psum = ctx.enter_context(tc.psum_pool(name="psum", bufs=1))
+
+        offs_t = keep.tile([P, S // 16], U16, name="offs_t")
+        me_t = keep.tile([P, U // 16], U16, name="me_t")
+        ot_t = keep.tile([P, U // 16], U16, name="ot_t")
+        xw = keep.tile([P, T], U32, name="xw", align_bytes=64)
+        xs = keep.tile([P, T], U8, name="xs", align_bytes=64)
+        w1w = keep.tile([P, 2 * H], U8, name="w1w", align_bytes=64)
+        w2w = keep.tile([P, 2 * H], U8, name="w2w", align_bytes=64)
+        w3w = keep.tile([P, 2 * N], U8, name="w3w", align_bytes=64)
+        w1s = keep.tile([P, H], U8, name="w1s", align_bytes=64)
+        w2s = keep.tile([P, H], U8, name="w2s", align_bytes=64)
+        w3s = keep.tile([P, N], U8, name="w3s", align_bytes=64)
+        unit_t = keep.tile([P, PACK], F32, name="unit_t")
+        neg_unit = keep.tile([P, PACK], F32, name="neg_unit")
+        ident = keep.tile([P, P], F32, name="ident")
+        banks = [psum.tile([P, 512], F32, name="bank%d" % b) for b in range(BANKS)]
+
+        def load_scales(queue, plane, rows):
+            for q in range(4):
+                queue.dma_start(out=plane[32 * q : 32 * q + 4, :].bitcast(I32), in_=rows[0, 4 * q : 4 * q + 4, :].bitcast(I32))
+
+        nc.vector.memset(xs[:].bitcast(I32), 0)
+        nc.vector.memset(w1s[:].bitcast(I32), 0)
+        nc.vector.memset(w2s[:].bitcast(I32), 0)
+        nc.vector.memset(w3s[:].bitcast(I32), 0)
+        nc.sync.dma_start(out=xw[:].bitcast(I32), in_=x_words[0].rearrange("p c r -> p (c r)").bitcast(I32))
+        nc.sync.dma_start(offs_t[:], offs)
+        load_scales(nc.scalar, xs, x_scales)
+        nc.sync.dma_start(out=w1w[:].bitcast(I32), in_=w1_words[0].bitcast(I32))
+        nc.sync.dma_start(out=w2w[:].bitcast(I32), in_=w2_words[0].bitcast(I32))
+        load_scales(nc.sync, w1s, w1_scales)
+        load_scales(nc.sync, w2s, w2_scales)
+        nc.sync.dma_start(ot_t[:], ot)
+        nc.sync.dma_start(me_t[:], me)
+        nc.sync.dma_start(out=unit_t[:], in_=unit.rearrange("(p t) o -> p (t o)", t=PACK))
+        nc.sync.dma_start(out=w3w[:].bitcast(I32), in_=w3_words[0].bitcast(I32))
+        load_scales(nc.sync, w3s, w3_scales)
+        make_identity(nc, ident[:])
+        nc.gpsimd.tensor_scalar(out=neg_unit[:], in0=unit_t[:], scalar1=-1.0, scalar2=0.0, op0=ALU.mult, op1=ALU.add)
+
+        xq_w = keep.tile([P, S], U32, name="xq_w", align_bytes=64)
+        xq_s = keep.tile([P, S], U8, name="xq_s", align_bytes=64)
+        nc.vector.tensor_copy(xq_s[:], xs[:].indirect(offs_t[:]))
+        nc.vector.tensor_copy(xq_w[:], xw[:].indirect(offs_t[:]))
+
+        px, vx = [], []
+        for b in range(BLOCKS):
+            for side, (words, scales, tables) in enumerate(((w1w, w1s, px), (w2w, w2s, vx))):
+                bank = banks[2 * b + side]
+                nc.tensor.matmul_mx(
+                    out=bank[:],
+                    lhsT=words[:, 2 * P * b : 2 * P * (b + 1)].bitcast(FP4X4),
+                    lhsT_scale=scales[:, P * b : P * (b + 1)],
+                    rhs=xq_w[:].bitcast(FP8X4),
+                    rhs_scale=xq_s[:],
+                    start=True,
+                    stop=True,
+                )
+                table = keep.tile([P, S], F32, name="table%d_%d" % (side, b))
+                if side == 0:
+                    nc.vector.tensor_copy(out=table[:], in_=bank[:])
+                else:
+                    nc.scalar.copy(out=table[:], in_=bank[:])
+                tables.append(table)
+
+        def dealt(bank):
+            return bank[:].rearrange("r (m t) -> r t m", t=PACK)
+
+        def by_tile(ap):
+            return ap.rearrange("r (t m) -> r t m", t=PACK)
+
+        d04 = keep.tile([P, CHUNKS, H], F32, name="d04")
+        cls = keep.tile([P, CHUNKS, H], F32, name="cls")
+        ttc = keep.tile([P, CHUNKS, H], F32, name="ttc")
+        fetched = keep.tile([P, 4 * BLOCKS, SPAN], F32, name="fetched")
+        sq_rec = keep.tile([P, PACK, H], F32, name="sq_rec")
+        logs = keep.tile([P, PACK, CHUNKS * P], F32, name="logs")
+        num = fetched[:].rearrange("r (c a) b -> r c (a b)", c=CHUNKS)
+
+        def turn(bank, t, source, start, stop):
+            nc.tensor.matmul(bank[:, P * t : P * (t + 1)], source, ident[:], start=start, stop=stop, is_transpose=True)
+
+        for s in range(SPANS):
+            cols = slice(s * SPAN // 16, (s + 1) * SPAN // 16)
+            chunks = range(s * SPAN // CHUNK, (s + 1) * SPAN // CHUNK)
+            dv = {c: banks[(2 * c) % BANKS] for c in chunks}
+            dx = {c: banks[(2 * c + 1) % BANKS] for c in chunks}
+            for side, (tables, plus, minus, diff) in enumerate(((vx, me_t, ot_t, dv), (px, ot_t, me_t, dx))):
+                for b in range(BLOCKS):
+                    pos = fetched[:, 2 * (BLOCKS * side + b), :]
+                    neg = fetched[:, 2 * (BLOCKS * side + b) + 1, :]
+                    nc.vector.tensor_copy(pos, tables[b][:].indirect(plus[:, cols]))
+                    nc.scalar.activation(neg, tables[b][:].indirect(minus[:, cols]), ACT.Copy, scale=-1.0)
+                    for c in chunks:
+                        rows = slice(c * CHUNK - s * SPAN, (c + 1) * CHUNK - s * SPAN)
+                        turn(diff[c], b, pos[:, rows], True, False)
+                        turn(diff[c], b, neg[:, rows], False, True)
+            for c in chunks:
+                nc.vector.tensor_scalar(out=by_tile(d04[:, c, :]), in0=dealt(dv[c]), scalar1=0.4, scalar2=None, op0=ALU.mult)
+            for c in chunks:
+                sq = sq_rec[:, :, P * (c % PACK) : P * (c % PACK + 1)]
+                nc.scalar.activation(sq, by_tile(d04[:, c, :]), ACT.Square, scale=2.5)
+                nc.scalar.activation(logs[:, :, P * c : P * (c + 1)], sq, ACT.Ln, bias=0.3)
+                nc.vector.scalar_tensor_tensor(
+                    out=by_tile(cls[:, c, :]), in0=dealt(dx[c]), scalar=2.5, in1=by_tile(d04[:, c, :]), op0=ALU.mult, op1=ALU.mult
+                )
+
+
+        for c in range(CHUNKS):
+            nc.vector.tensor_scalar(out=num[:, c, :], in0=cls[:, c, :], scalar1=0.0, scalar2=0.1, op0=ALU.max, op1=ALU.add)
+        for c in range(CHUNKS):
+            for t in range(PACK):
+                turn(banks[c], t, d04[:, c, P * t : P * (t + 1)], t == 0, False)
+        for c in range(CHUNKS):
+            rec = sq_rec[:, c % PACK, :]
+            nc.scalar.activation(by_tile(rec), logs[:, :, P * c : P * (c + 1)], ACT.Exp, scale=-1.0)
+            nc.vector.tensor_tensor(out=ttc[:, c, :], in0=num[:, c, :], in1=rec, op=ALU.mult)
+            for t in range(PACK):
+                turn(banks[c], t, ttc[:, c, P * t : P * (t + 1)], False, False)
+        for c in range(4):
+            nc.vector.tensor_tensor(out=cls[:, c, :], in0=ttc[:, c, :], in1=ttc[:, c, :], op=ALU.mult)
+
+        for s in range(SPANS):
+            hid = ring.tile([P, SPAN * PACK], BF16, name="hid", align_bytes=64)
+            for c in range(s * SPAN // CHUNK, (s + 1) * SPAN // CHUNK):
+                if c >= 4:
+                    nc.scalar.activation(cls[:, c, :], ttc[:, c, :], ACT.Square)
+                lg = logs[:, c % PACK, H : 2 * H]
+                nc.scalar.activation(lg, cls[:, c, :], ACT.Ln, bias=0.3)
+                for t in range(PACK):
+                    turn(banks[c], t, lg[:, P * t : P * (t + 1)], False, t == PACK - 1)
+                first = (c * CHUNK - s * SPAN) * PACK
+                nc.vector.tensor_tensor(
+                    out=hid[:, first : first + CHUNK * PACK].rearrange("p (r t) -> p r t", t=PACK),
+                    in0=banks[c][:].rearrange("p (t r) -> p r t", t=PACK),
+                    in1=neg_unit[:].unsqueeze(1).to_broadcast([P, CHUNK, PACK]),
+                    op=ALU.mult,
+                )
+            codes = ring.tile([P, SPAN], U32, name="codes", align_bytes=64)
+            scales = ring.tile([P, SPAN], U8, name="scales", align_bytes=64)
+            nc.vector.quantize_mx(out=codes[:].bitcast(FP8X4), scales=scales[:], in_=hid[:])
+            acc = banks[2 * s][:, 0:SPAN]
+            nc.tensor.matmul_mx(
+                out=acc, lhsT=w3w[:].bitcast(FP4X4), lhsT_scale=w3s[:], rhs=codes[:].bitcast(FP8X4), rhs_scale=scales[:],
+                start=True, stop=True,
+            )
+            res = ring.tile([P, SPAN], F32, name="res")
+            nc.scalar.copy(out=res[:], in_=acc)
+            nc.sync.dma_start(out=out[:, s * SPAN : (s + 1) * SPAN], in_=res[:])

@@ -57,18 +57,18 @@ def tile_picked_yttcpl_log_p_kernel(
                 queue.dma_start(out=plane[32 * q : 32 * q + 4, :].bitcast(I32), in_=rows[0, 4 * q : 4 * q + 4, :].bitcast(I32))
 
         nc.vector.memset(xs[:].bitcast(I32), 0)
-        nc.vector.memset(w1s[:].bitcast(I32), 0)
         nc.vector.memset(w2s[:].bitcast(I32), 0)
+        nc.vector.memset(w1s[:].bitcast(I32), 0)
         nc.vector.memset(w3s[:].bitcast(I32), 0)
         nc.sync.dma_start(out=xw[:].bitcast(I32), in_=x_words[0].rearrange("p c r -> p (c r)").bitcast(I32))
         nc.sync.dma_start(offs_t[:], offs)
         load_scales(nc.scalar, xs, x_scales)
-        nc.sync.dma_start(out=w1w[:].bitcast(I32), in_=w1_words[0].bitcast(I32))
         nc.sync.dma_start(out=w2w[:].bitcast(I32), in_=w2_words[0].bitcast(I32))
-        load_scales(nc.sync, w1s, w1_scales)
         load_scales(nc.sync, w2s, w2_scales)
         nc.sync.dma_start(ot_t[:], ot)
         nc.sync.dma_start(me_t[:], me)
+        nc.sync.dma_start(out=w1w[:].bitcast(I32), in_=w1_words[0].bitcast(I32))
+        load_scales(nc.sync, w1s, w1_scales)
         nc.sync.dma_start(out=unit_t[:], in_=unit.rearrange("(p t) o -> p (t o)", t=PACK))
         nc.sync.dma_start(out=w3w[:].bitcast(I32), in_=w3_words[0].bitcast(I32))
         load_scales(nc.sync, w3s, w3_scales)
@@ -80,25 +80,19 @@ def tile_picked_yttcpl_log_p_kernel(
         nc.vector.tensor_copy(xq_s[:], xs[:].indirect(offs_t[:]))
         nc.vector.tensor_copy(xq_w[:], xw[:].indirect(offs_t[:]))
 
-        px, vx = [], []
-        for b in range(BLOCKS):
-            for side, (words, scales, tables) in enumerate(((w1w, w1s, px), (w2w, w2s, vx))):
-                bank = banks[2 * b + side]
-                nc.tensor.matmul_mx(
-                    out=bank[:],
-                    lhsT=words[:, 2 * P * b : 2 * P * (b + 1)].bitcast(FP4X4),
-                    lhsT_scale=scales[:, P * b : P * (b + 1)],
-                    rhs=xq_w[:].bitcast(FP8X4),
-                    rhs_scale=xq_s[:],
-                    start=True,
-                    stop=True,
-                )
-                table = keep.tile([P, S], F32, name="table%d_%d" % (side, b))
-                if side == 0:
-                    nc.vector.tensor_copy(out=table[:], in_=bank[:])
-                else:
-                    nc.scalar.copy(out=table[:], in_=bank[:])
-                tables.append(table)
+        def product(bank, words, plane, b):
+            nc.tensor.matmul_mx(
+                out=bank[:],
+                lhsT=words[:, 2 * P * b : 2 * P * (b + 1)].bitcast(FP4X4),
+                lhsT_scale=plane[:, P * b : P * (b + 1)],
+                rhs=xq_w[:].bitcast(FP8X4),
+                rhs_scale=xq_s[:],
+                start=True,
+                stop=True,
+            )
+
+        def turn(bank, t, source, start, stop):
+            nc.tensor.matmul(bank[:, P * t : P * (t + 1)], source, ident[:], start=start, stop=stop, is_transpose=True)
 
         def dealt(bank):
             return bank[:].rearrange("r (m t) -> r t m", t=PACK)
@@ -106,77 +100,94 @@ def tile_picked_yttcpl_log_p_kernel(
         def by_tile(ap):
             return ap.rearrange("r (t m) -> r t m", t=PACK)
 
-        d04 = keep.tile([P, CHUNKS, H], F32, name="d04")
-        cls = keep.tile([P, CHUNKS, H], F32, name="cls")
-        ttc = keep.tile([P, CHUNKS, H], F32, name="ttc")
-        fetched = keep.tile([P, 4 * BLOCKS, SPAN], F32, name="fetched")
-        sq_rec = keep.tile([P, PACK, H], F32, name="sq_rec")
-        logs = keep.tile([P, PACK, CHUNKS * P], F32, name="logs")
-        num = fetched[:].rearrange("r (c a) b -> r c (a b)", c=CHUNKS)
+        def in_eighths(ap):
+            return ap.rearrange("r (a m) -> r a m", a=CHUNKS)
 
-        def turn(bank, t, source, start, stop):
-            nc.tensor.matmul(bank[:, P * t : P * (t + 1)], source, ident[:], start=start, stop=stop, is_transpose=True)
+        d04 = keep.tile([P, CHUNKS, H], F32, name="d04")
+        pos = keep.tile([P, 1, BLOCKS, SPAN], F32, name="pos")
+        neg = keep.tile([P, 2, SPANS, BLOCKS, SPAN], F32, name="neg")
+        rec = keep.tile([P, CHUNKS, H], F32, name="rec")
+        num = keep.tile([P, CHUNKS, H], F32, name="num")
+        ttc = keep.tile([P, CHUNKS, H], F32, name="ttc")
+        logs = keep.tile([P, PACK, CHUNKS * P], F32, name="logs")
+
+        def differences(side, s, tables, plus, minus):
+            cols = slice(s * SPAN // 16, (s + 1) * SPAN // 16)
+            for b in range(BLOCKS):
+                nc.vector.tensor_copy(pos[:, s % 1, b, :], tables[b][:].indirect(plus[:, cols]))
+                nc.scalar.activation(neg[:, side, s, b, :], tables[b][:].indirect(minus[:, cols]), ACT.Copy, scale=-1.0)
+                for h in range(SPAN // CHUNK):
+                    bank = banks[(2 * s + h) % 4]
+                    turn(bank, b, pos[:, s % 1, b, CHUNK * h : CHUNK * (h + 1)], True, False)
+                    turn(bank, b, neg[:, side, s, b, CHUNK * h : CHUNK * (h + 1)], False, True)
+
+        vx, px = [], []
+        for b in range(BLOCKS):
+            product(banks[b], w2w, w2s, b)
+            table = keep.tile([P, S], F32, name="vx%d" % b)
+            if b % 2 == 0:
+                nc.scalar.copy(out=table[:], in_=banks[b][:])
+            else:
+                nc.vector.tensor_copy(out=table[:], in_=banks[b][:])
+            vx.append(table)
+        for b in range(BLOCKS):
+            product(banks[4 + b], w1w, w1s, b)
+            table = keep.tile([P, S], F32, name="px%d" % b)
+            nc.vector.tensor_copy(out=table[:], in_=banks[4 + b][:])
+            px.append(table)
 
         for s in range(SPANS):
-            cols = slice(s * SPAN // 16, (s + 1) * SPAN // 16)
-            chunks = range(s * SPAN // CHUNK, (s + 1) * SPAN // CHUNK)
-            dv = {c: banks[(2 * c) % BANKS] for c in chunks}
-            dx = {c: banks[(2 * c + 1) % BANKS] for c in chunks}
-            for side, (tables, plus, minus, diff) in enumerate(((vx, me_t, ot_t, dv), (px, ot_t, me_t, dx))):
-                for b in range(BLOCKS):
-                    pos = fetched[:, 2 * (BLOCKS * side + b), :]
-                    neg = fetched[:, 2 * (BLOCKS * side + b) + 1, :]
-                    nc.vector.tensor_copy(pos, tables[b][:].indirect(plus[:, cols]))
-                    nc.scalar.activation(neg, tables[b][:].indirect(minus[:, cols]), ACT.Copy, scale=-1.0)
-                    for c in chunks:
-                        rows = slice(c * CHUNK - s * SPAN, (c + 1) * CHUNK - s * SPAN)
-                        turn(diff[c], b, pos[:, rows], True, False)
-                        turn(diff[c], b, neg[:, rows], False, True)
-            for c in chunks:
-                nc.vector.tensor_scalar(out=by_tile(d04[:, c, :]), in0=dealt(dv[c]), scalar1=0.4, scalar2=None, op0=ALU.mult)
-            for c in chunks:
-                sq = sq_rec[:, :, P * (c % PACK) : P * (c % PACK + 1)]
-                nc.scalar.activation(sq, by_tile(d04[:, c, :]), ACT.Square, scale=2.5)
-                nc.scalar.activation(logs[:, :, P * c : P * (c + 1)], sq, ACT.Ln, bias=0.3)
-                nc.vector.scalar_tensor_tensor(
-                    out=by_tile(cls[:, c, :]), in0=dealt(dx[c]), scalar=2.5, in1=by_tile(d04[:, c, :]), op0=ALU.mult, op1=ALU.mult
+            differences(0, s, vx, me_t, ot_t)
+            for c in (2 * s, 2 * s + 1):
+                nc.vector.tensor_scalar(out=by_tile(d04[:, c, :]), in0=dealt(banks[c % 4]), scalar1=0.4, scalar2=None, op0=ALU.mult)
+            for c in (2 * s, 2 * s + 1):
+                sq = rec[:, :, 64 * c : 64 * (c + 1)]
+                nc.gpsimd.tensor_tensor(out=sq, in0=in_eighths(d04[:, c, :]), in1=in_eighths(d04[:, c, :]), op=ALU.mult)
+                nc.scalar.activation(
+                    logs[:, :, P * c : P * (c + 1)].rearrange("r t (u m) -> r t u m", u=2),
+                    sq.rearrange("r (t u) m -> r t u m", u=2), ACT.Ln, bias=0.3, scale=6.25,
                 )
+        total = [banks[(c + 4) % BANKS] for c in range(CHUNKS)]
 
+        def add_term(c, term, start, stop):
+            for t in range(PACK):
+                turn(total[c], t, term[:, P * t : P * (t + 1)], start and t == 0, stop and t == PACK - 1)
 
+        for s in range(SPANS):
+            differences(1, s, px, ot_t, me_t)
+            for c in (2 * s, 2 * s + 1):
+                cls = ring.tile([P, H], F32, name="cls", bufs=2)
+                nc.vector.scalar_tensor_tensor(
+                    out=by_tile(cls[:]), in0=dealt(banks[c % 4]), scalar=2.5, in1=by_tile(d04[:, c, :]), op0=ALU.mult, op1=ALU.mult
+                )
+                nc.gpsimd.tensor_scalar(out=num[:, c, :], in0=cls[:], scalar1=0.0, scalar2=0.1, op0=ALU.max, op1=ALU.add)
+            add_term(s, d04[:, s, :], True, False)
+        for c in range(CHUNKS // 2, CHUNKS):
+            add_term(c, d04[:, c, :], True, False)
         for c in range(CHUNKS):
-            nc.vector.tensor_scalar(out=num[:, c, :], in0=cls[:, c, :], scalar1=0.0, scalar2=0.1, op0=ALU.max, op1=ALU.add)
-        for c in range(CHUNKS):
-            for t in range(PACK):
-                turn(banks[c], t, d04[:, c, P * t : P * (t + 1)], t == 0, False)
-        for c in range(CHUNKS):
-            rec = sq_rec[:, c % PACK, :]
-            nc.scalar.activation(by_tile(rec), logs[:, :, P * c : P * (c + 1)], ACT.Exp, scale=-1.0)
-            nc.vector.tensor_tensor(out=ttc[:, c, :], in0=num[:, c, :], in1=rec, op=ALU.mult)
-            for t in range(PACK):
-                turn(banks[c], t, ttc[:, c, P * t : P * (t + 1)], False, False)
-        for c in range(4):
-            nc.vector.tensor_tensor(out=cls[:, c, :], in0=ttc[:, c, :], in1=ttc[:, c, :], op=ALU.mult)
+            nc.scalar.activation(by_tile(rec[:, c, :]), logs[:, :, P * c : P * (c + 1)], ACT.Exp, scale=-1.0)
+            nc.vector.tensor_tensor(out=ttc[:, c, :], in0=num[:, c, :], in1=rec[:, c, :], op=ALU.mult)
+            add_term(c, ttc[:, c, :], False, False)
 
         for s in range(SPANS):
             hid = ring.tile([P, SPAN * PACK], BF16, name="hid", align_bytes=64)
-            for c in range(s * SPAN // CHUNK, (s + 1) * SPAN // CHUNK):
-                if c >= 4:
-                    nc.scalar.activation(cls[:, c, :], ttc[:, c, :], ACT.Square)
+            for c in (2 * s, 2 * s + 1):
+                t2 = rec[:, c, :]
+                nc.scalar.activation(t2, ttc[:, c, :], ACT.Square)
                 lg = logs[:, c % PACK, H : 2 * H]
-                nc.scalar.activation(lg, cls[:, c, :], ACT.Ln, bias=0.3)
-                for t in range(PACK):
-                    turn(banks[c], t, lg[:, P * t : P * (t + 1)], False, t == PACK - 1)
-                first = (c * CHUNK - s * SPAN) * PACK
+                nc.scalar.activation(lg, t2, ACT.Ln, bias=0.3)
+                add_term(c, lg, False, True)
+                first = (c - 2 * s) * CHUNK * PACK
                 nc.vector.tensor_tensor(
                     out=hid[:, first : first + CHUNK * PACK].rearrange("p (r t) -> p r t", t=PACK),
-                    in0=banks[c][:].rearrange("p (t r) -> p r t", t=PACK),
+                    in0=total[c][:].rearrange("p (t r) -> p r t", t=PACK),
                     in1=neg_unit[:].unsqueeze(1).to_broadcast([P, CHUNK, PACK]),
                     op=ALU.mult,
                 )
             codes = ring.tile([P, SPAN], U32, name="codes", align_bytes=64)
             scales = ring.tile([P, SPAN], U8, name="scales", align_bytes=64)
             nc.vector.quantize_mx(out=codes[:].bitcast(FP8X4), scales=scales[:], in_=hid[:])
-            acc = banks[2 * s][:, 0:SPAN]
+            acc = total[2 * s][:, 0:SPAN]
             nc.tensor.matmul_mx(
                 out=acc, lhsT=w3w[:].bitcast(FP4X4), lhsT_scale=w3s[:], rhs=codes[:].bitcast(FP8X4), rhs_scale=scales[:],
                 start=True, stop=True,

@@ -52,28 +52,28 @@ def tile_picked_yttcpl_log_p_kernel(
         ident = keep.tile([P, P], F32, name="ident")
         banks = [psum.tile([P, 512], F32, name="bank%d" % b) for b in range(BANKS)]
 
-        def load_scales(queue, plane, rows):
-            for q in range(4):
-                queue.dma_start(out=plane[32 * q : 32 * q + 4, :].bitcast(I32), in_=rows[0, 4 * q : 4 * q + 4, :].bitcast(I32))
+        def load_rows(queue, plane, rows, q):
+            queue.dma_start(out=plane[32 * q : 32 * q + 4, :].bitcast(I32), in_=rows[0, 4 * q : 4 * q + 4, :].bitcast(I32))
 
-        nc.vector.memset(xs[:].bitcast(I32), 0)
-        nc.vector.memset(w2s[:].bitcast(I32), 0)
-        nc.vector.memset(w1s[:].bitcast(I32), 0)
-        nc.vector.memset(w3s[:].bitcast(I32), 0)
+        for plane in (xs, w2s, w1s, w3s):
+            nc.vector.memset(plane[:].bitcast(I32), 0)
         nc.sync.dma_start(out=xw[:].bitcast(I32), in_=x_words[0].rearrange("p c r -> p (c r)").bitcast(I32))
         nc.sync.dma_start(offs_t[:], offs)
-        load_scales(nc.scalar, xs, x_scales)
+        for q in range(4):
+            load_rows(nc.scalar, xs, x_scales, q)
         nc.sync.dma_start(out=w2w[:].bitcast(I32), in_=w2_words[0].bitcast(I32))
-        load_scales(nc.sync, w2s, w2_scales)
+        for q in range(4):
+            load_rows(nc.sync, w2s, w2_scales, q)
         nc.sync.dma_start(ot_t[:], ot)
         nc.sync.dma_start(me_t[:], me)
         nc.sync.dma_start(out=w1w[:].bitcast(I32), in_=w1_words[0].bitcast(I32))
-        load_scales(nc.sync, w1s, w1_scales)
+        for q in range(4):
+            load_rows(nc.sync, w1s, w1_scales, q)
         nc.sync.dma_start(out=unit_t[:], in_=unit.rearrange("(p t) o -> p (t o)", t=PACK))
         nc.sync.dma_start(out=w3w[:].bitcast(I32), in_=w3_words[0].bitcast(I32))
-        load_scales(nc.sync, w3s, w3_scales)
+        for q in range(4):
+            load_rows(nc.sync, w3s, w3_scales, q)
         make_identity(nc, ident[:])
-        nc.gpsimd.tensor_scalar(out=neg_unit[:], in0=unit_t[:], scalar1=-1.0, scalar2=0.0, op0=ALU.mult, op1=ALU.add)
 
         xq_w = keep.tile([P, S], U32, name="xq_w", align_bytes=64)
         xq_s = keep.tile([P, S], U8, name="xq_s", align_bytes=64)
@@ -100,98 +100,121 @@ def tile_picked_yttcpl_log_p_kernel(
         def by_tile(ap):
             return ap.rearrange("r (t m) -> r t m", t=PACK)
 
-        def in_eighths(ap):
-            return ap.rearrange("r (a m) -> r a m", a=CHUNKS)
+        def in_rows(ap, a):
+            return ap.rearrange("r (a m) -> r a m", a=a)
 
-        d04 = keep.tile([P, CHUNKS, H], F32, name="d04")
-        pos = keep.tile([P, 1, BLOCKS, SPAN], F32, name="pos")
-        neg = keep.tile([P, 2, SPANS, BLOCKS, SPAN], F32, name="neg")
-        rec = keep.tile([P, CHUNKS, H], F32, name="rec")
-        num = keep.tile([P, CHUNKS, H], F32, name="num")
-        ttc = keep.tile([P, CHUNKS, H], F32, name="ttc")
-        logs = keep.tile([P, PACK, CHUNKS * P], F32, name="logs")
+        GV, GS = (256, 256), 512
+        d04 = keep.tile([P, CHUNKS * H], F32, name="d04")
+        pos = keep.tile([P, BLOCKS, max(GV)], F32, name="pos")
+        neg = keep.tile([P, 2, BLOCKS, U], F32, name="neg")
+        rec = keep.tile([P, SPANS, 2 * H], F32, name="rec")
+        logs = neg[:, 0]
+        log_den = logs.rearrange("r b (k s m) -> r s b k m", k=SPANS, s=SPANS)
+        num = keep.tile([P, SPANS, 2 * H], F32, name="num")
+        ttc = [neg[:, 1, :, SPAN * ((s + 2) % SPANS) : SPAN * ((s + 2) % SPANS + 1)] for s in range(SPANS)]
 
-        def differences(side, s, tables, plus, minus):
-            cols = slice(s * SPAN // 16, (s + 1) * SPAN // 16)
+        def differences(side, g, tables, plus, minus):
             for b in range(BLOCKS):
-                nc.vector.tensor_copy(pos[:, s % 1, b, :], tables[b][:].indirect(plus[:, cols]))
-                nc.scalar.activation(neg[:, side, s, b, :], tables[b][:].indirect(minus[:, cols]), ACT.Copy, scale=-1.0)
-                for h in range(SPAN // CHUNK):
-                    bank = banks[(2 * s + h) % 4]
-                    turn(bank, b, pos[:, s % 1, b, CHUNK * h : CHUNK * (h + 1)], True, False)
-                    turn(bank, b, neg[:, side, s, b, CHUNK * h : CHUNK * (h + 1)], False, True)
+                r0, w = g * GV[side], GV[side]
+                nc.vector.tensor_copy(pos[:, b, :w], tables[b][:].indirect(plus[:, r0 // 16 : (r0 + w) // 16]))
+                if r0 % GS == 0:
+                    nc.scalar.activation(
+                        neg[:, side, b, r0 : r0 + GS], tables[b][:].indirect(minus[:, r0 // 16 : (r0 + GS) // 16]), ACT.Copy, scale=-1.0
+                    )
+                for r in range(r0, r0 + w, CHUNK):
+                    bank = banks[(r // CHUNK) % 4]
+                    turn(bank, b, pos[:, b, r - r0 : r - r0 + CHUNK], True, False)
+                    turn(bank, b, neg[:, side, b, r : r + CHUNK], False, True)
 
         vx, px = [], []
         for b in range(BLOCKS):
             product(banks[b], w2w, w2s, b)
-            table = keep.tile([P, S], F32, name="vx%d" % b)
+            table = keep.tile([P, S + 16], F32, name="vx%d" % b)
+            nc.gpsimd.memset(table[:, S:], 0.0)
             if b % 2 == 0:
-                nc.scalar.copy(out=table[:], in_=banks[b][:])
+                nc.scalar.copy(out=table[:, :S], in_=banks[b][:])
             else:
-                nc.vector.tensor_copy(out=table[:], in_=banks[b][:])
+                nc.vector.tensor_copy(out=table[:, :S], in_=banks[b][:])
             vx.append(table)
         for b in range(BLOCKS):
             product(banks[4 + b], w1w, w1s, b)
-            table = keep.tile([P, S], F32, name="px%d" % b)
-            nc.vector.tensor_copy(out=table[:], in_=banks[4 + b][:])
+            table = keep.tile([P, S + 16], F32, name="px%d" % b)
+            nc.gpsimd.memset(table[:, S:], 0.0)
+            if b < 2:
+                nc.scalar.copy(out=table[:, :S], in_=banks[4 + b][:])
+            else:
+                nc.vector.tensor_copy(out=table[:, :S], in_=banks[4 + b][:])
             px.append(table)
+        nc.gpsimd.tensor_scalar(out=neg_unit[:], in0=unit_t[:], scalar1=-1.0, scalar2=0.0, op0=ALU.mult, op1=ALU.add)
 
+        for g in range(U // GV[0]):
+            differences(0, g, vx, me_t, ot_t)
+            for s in range(g * GV[0] // SPAN, (g + 1) * GV[0] // SPAN):
+                for c in (2 * s, 2 * s + 1):
+                    nc.vector.tensor_scalar(out=by_tile(d04[:, H * c : H * (c + 1)]), in0=dealt(banks[c % 4]), scalar1=0.4, scalar2=None, op0=ALU.mult)
+                    half = in_rows(d04[:, H * c : H * (c + 1)], 2)
+                    nc.gpsimd.tensor_tensor(out=rec[:, 2 * (c % 2) : 2 * (c % 2) + 2, 256 * s : 256 * (s + 1)], in0=half, in1=half, op=ALU.mult)
         for s in range(SPANS):
-            differences(0, s, vx, me_t, ot_t)
-            for c in (2 * s, 2 * s + 1):
-                nc.vector.tensor_scalar(out=by_tile(d04[:, c, :]), in0=dealt(banks[c % 4]), scalar1=0.4, scalar2=None, op0=ALU.mult)
-            for c in (2 * s, 2 * s + 1):
-                sq = rec[:, :, 64 * c : 64 * (c + 1)]
-                nc.gpsimd.tensor_tensor(out=sq, in0=in_eighths(d04[:, c, :]), in1=in_eighths(d04[:, c, :]), op=ALU.mult)
-                nc.scalar.activation(
-                    logs[:, :, P * c : P * (c + 1)].rearrange("r t (u m) -> r t u m", u=2),
-                    sq.rearrange("r (t u) m -> r t u m", u=2), ACT.Ln, bias=0.3, scale=6.25,
-                )
+            nc.scalar.activation(log_den[:, s], rec[:, :, 256 * s : 256 * (s + 1)].rearrange("r b (k m) -> r b k m", k=SPANS), ACT.Ln, bias=0.3, scale=6.25)
         total = [banks[(c + 4) % BANKS] for c in range(CHUNKS)]
 
         def add_term(c, term, start, stop):
             for t in range(PACK):
                 turn(total[c], t, term[:, P * t : P * (t + 1)], start and t == 0, stop and t == PACK - 1)
 
-        for s in range(SPANS):
+        def closing(s):
             differences(1, s, px, ot_t, me_t)
+            cls = ring.tile([P, 2 * H], F32, name="cls")
             for c in (2 * s, 2 * s + 1):
-                cls = ring.tile([P, H], F32, name="cls", bufs=2)
                 nc.vector.scalar_tensor_tensor(
-                    out=by_tile(cls[:]), in0=dealt(banks[c % 4]), scalar=2.5, in1=by_tile(d04[:, c, :]), op0=ALU.mult, op1=ALU.mult
+                    out=by_tile(cls[:, H * (c % 2) : H * (c % 2 + 1)]), in0=dealt(banks[c % 4]), scalar=2.5,
+                    in1=by_tile(d04[:, H * c : H * (c + 1)]), op0=ALU.mult, op1=ALU.mult,
                 )
-                nc.gpsimd.tensor_scalar(out=num[:, c, :], in0=cls[:], scalar1=0.0, scalar2=0.1, op0=ALU.max, op1=ALU.add)
-            add_term(s, d04[:, s, :], True, False)
-        for c in range(CHUNKS // 2, CHUNKS):
-            add_term(c, d04[:, c, :], True, False)
-        for c in range(CHUNKS):
-            nc.scalar.activation(by_tile(rec[:, c, :]), logs[:, :, P * c : P * (c + 1)], ACT.Exp, scale=-1.0)
-            nc.vector.tensor_tensor(out=ttc[:, c, :], in0=num[:, c, :], in1=rec[:, c, :], op=ALU.mult)
-            add_term(c, ttc[:, c, :], False, False)
+            nc.vector.tensor_scalar(out=num[:, s, :], in0=cls[:], scalar1=0.0, scalar2=0.1, op0=ALU.max, op1=ALU.add)
+            add_term(s, d04[:, H * s : H * (s + 1)], True, False)
 
-        for s in range(SPANS):
-            hid = ring.tile([P, SPAN * PACK], BF16, name="hid", align_bytes=64)
+        def time_to_collision(s):
+            nc.vector.tensor_tensor(out=ttc[s], in0=in_rows(num[:, s, :], 4), in1=in_rows(rec[:, s, :], 4), op=ALU.mult)
             for c in (2 * s, 2 * s + 1):
-                t2 = rec[:, c, :]
-                nc.scalar.activation(t2, ttc[:, c, :], ACT.Square)
-                lg = logs[:, c % PACK, H : 2 * H]
-                nc.scalar.activation(lg, t2, ACT.Ln, bias=0.3)
-                add_term(c, lg, False, True)
-                first = (c - 2 * s) * CHUNK * PACK
+                if c >= CHUNKS // 2:
+                    add_term(c, d04[:, H * c : H * (c + 1)], True, False)
+                for t in range(PACK):
+                    turn(total[c], t, ttc[s][:, 2 * (c % 2) + t // 2, P * (t % 2) : P * (t % 2 + 1)], False, False)
+
+        for s in range(SPANS - 1):
+            closing(s)
+        for s in range(SPANS):
+            nc.scalar.activation(rec[:, s, :].rearrange("r (b k m) -> r b k m", b=BLOCKS, k=SPANS), log_den[:, s], ACT.Exp, scale=-1.0)
+        time_to_collision(0)
+        closing(SPANS - 1)
+        for s in range(1, SPANS):
+            time_to_collision(s)
+
+        def finish(chunks):
+            s, n = chunks[0] // 2, len(chunks)
+            cols = slice(H * (chunks[0] % 2), H * (chunks[0] % 2 + n))
+            nc.scalar.activation(in_rows(rec[:, s, :], 4), ttc[s], ACT.Square)
+            nc.scalar.activation(logs[:, s, cols], rec[:, s, cols], ACT.Ln, bias=0.3)
+            hid = ring.tile([P, n * H], BF16, name="hid", align_bytes=64)
+            for k, c in enumerate(chunks):
+                add_term(c, logs[:, s, H * (c % 2) : H * (c % 2 + 1)], False, True)
                 nc.vector.tensor_tensor(
-                    out=hid[:, first : first + CHUNK * PACK].rearrange("p (r t) -> p r t", t=PACK),
+                    out=hid[:, k * H : (k + 1) * H].rearrange("p (r t) -> p r t", t=PACK),
                     in0=total[c][:].rearrange("p (t r) -> p r t", t=PACK),
                     in1=neg_unit[:].unsqueeze(1).to_broadcast([P, CHUNK, PACK]),
                     op=ALU.mult,
                 )
-            codes = ring.tile([P, SPAN], U32, name="codes", align_bytes=64)
-            scales = ring.tile([P, SPAN], U8, name="scales", align_bytes=64)
+            codes = ring.tile([P, n * CHUNK], U32, name="codes", align_bytes=64)
+            scales = ring.tile([P, n * CHUNK], U8, name="scales", align_bytes=64)
             nc.vector.quantize_mx(out=codes[:].bitcast(FP8X4), scales=scales[:], in_=hid[:])
-            acc = total[2 * s][:, 0:SPAN]
+            acc = total[chunks[0]][:, 0 : n * CHUNK]
             nc.tensor.matmul_mx(
                 out=acc, lhsT=w3w[:].bitcast(FP4X4), lhsT_scale=w3s[:], rhs=codes[:].bitcast(FP8X4), rhs_scale=scales[:],
                 start=True, stop=True,
             )
-            res = ring.tile([P, SPAN], F32, name="res")
+            res = ring.tile([P, n * CHUNK], F32, name="res", bufs=4)
             nc.scalar.copy(out=res[:], in_=acc)
-            nc.sync.dma_start(out=out[:, s * SPAN : (s + 1) * SPAN], in_=res[:])
+            nc.sync.dma_start(out=out[:, chunks[0] * CHUNK : (chunks[0] + n) * CHUNK], in_=res[:])
+
+        for chunks in ((0, 1), (2, 3), (4, 5), (6, 7)):
+            finish(chunks)

@@ -73,6 +73,9 @@ def tile_picked_yttcpl_log_p_kernel(
         nc.sync.dma_start(out=w3w[:].bitcast(I32), in_=w3_words[0].bitcast(I32))
         for q in range(4):
             load_rows(nc.sync, w3s, w3_scales, q)
+        warm = keep.tile([P, 2], F32, name="warm")
+        nc.gpsimd.memset(warm[:, 0:1], 1.0)
+        nc.scalar.activation(warm[:, 1:2], warm[:, 0:1], ACT.Ln)
         make_identity(nc, ident[:])
 
         xq_w = keep.tile([P, S], U32, name="xq_w", align_bytes=64)
@@ -103,7 +106,7 @@ def tile_picked_yttcpl_log_p_kernel(
         def in_rows(ap, a):
             return ap.rearrange("r (a m) -> r a m", a=a)
 
-        GV, GS = (256, 256), 512
+        GV, GS = (512, 256), 512
         d04 = keep.tile([P, CHUNKS * H], F32, name="d04")
         pos = keep.tile([P, BLOCKS, max(GV)], F32, name="pos")
         neg = keep.tile([P, 2, BLOCKS, U], F32, name="neg")
@@ -140,7 +143,7 @@ def tile_picked_yttcpl_log_p_kernel(
             product(banks[4 + b], w1w, w1s, b)
             table = keep.tile([P, S + 16], F32, name="px%d" % b)
             nc.gpsimd.memset(table[:, S:], 0.0)
-            if b < 2:
+            if b < 3:
                 nc.scalar.copy(out=table[:, :S], in_=banks[4 + b][:])
             else:
                 nc.vector.tensor_copy(out=table[:, :S], in_=banks[4 + b][:])
@@ -195,26 +198,28 @@ def tile_picked_yttcpl_log_p_kernel(
             cols = slice(H * (chunks[0] % 2), H * (chunks[0] % 2 + n))
             nc.scalar.activation(in_rows(rec[:, s, :], 4), ttc[s], ACT.Square)
             nc.scalar.activation(logs[:, s, cols], rec[:, s, cols], ACT.Ln, bias=0.3)
-            hid = ring.tile([P, n * H], BF16, name="hid", align_bytes=64)
-            for k, c in enumerate(chunks):
-                add_term(c, logs[:, s, H * (c % 2) : H * (c % 2 + 1)], False, True)
-                nc.vector.tensor_tensor(
-                    out=hid[:, k * H : (k + 1) * H].rearrange("p (r t) -> p r t", t=PACK),
-                    in0=total[c][:].rearrange("p (t r) -> p r t", t=PACK),
-                    in1=neg_unit[:].unsqueeze(1).to_broadcast([P, CHUNK, PACK]),
-                    op=ALU.mult,
+            for chunks in ([chunks] if s < SPANS - 1 else [(c,) for c in chunks]):
+                n = len(chunks)
+                hid = ring.tile([P, n * H], BF16, name="hid", align_bytes=64)
+                for k, c in enumerate(chunks):
+                    add_term(c, logs[:, s, H * (c % 2) : H * (c % 2 + 1)], False, True)
+                    nc.vector.tensor_tensor(
+                        out=hid[:, k * H : (k + 1) * H].rearrange("p (r t) -> p r t", t=PACK),
+                        in0=total[c][:].rearrange("p (t r) -> p r t", t=PACK),
+                        in1=neg_unit[:].unsqueeze(1).to_broadcast([P, CHUNK, PACK]),
+                        op=ALU.mult,
+                    )
+                codes = ring.tile([P, n * CHUNK], U32, name="codes", align_bytes=64)
+                scales = ring.tile([P, n * CHUNK], U8, name="scales", align_bytes=64)
+                nc.vector.quantize_mx(out=codes[:].bitcast(FP8X4), scales=scales[:], in_=hid[:])
+                acc = total[chunks[0]][:, 0 : n * CHUNK]
+                nc.tensor.matmul_mx(
+                    out=acc, lhsT=w3w[:].bitcast(FP4X4), lhsT_scale=w3s[:], rhs=codes[:].bitcast(FP8X4), rhs_scale=scales[:],
+                    start=True, stop=True,
                 )
-            codes = ring.tile([P, n * CHUNK], U32, name="codes", align_bytes=64)
-            scales = ring.tile([P, n * CHUNK], U8, name="scales", align_bytes=64)
-            nc.vector.quantize_mx(out=codes[:].bitcast(FP8X4), scales=scales[:], in_=hid[:])
-            acc = total[chunks[0]][:, 0 : n * CHUNK]
-            nc.tensor.matmul_mx(
-                out=acc, lhsT=w3w[:].bitcast(FP4X4), lhsT_scale=w3s[:], rhs=codes[:].bitcast(FP8X4), rhs_scale=scales[:],
-                start=True, stop=True,
-            )
-            res = ring.tile([P, n * CHUNK], F32, name="res", bufs=4)
-            nc.scalar.copy(out=res[:], in_=acc)
-            nc.sync.dma_start(out=out[:, chunks[0] * CHUNK : (chunks[0] + n) * CHUNK], in_=res[:])
+                res = ring.tile([P, n * CHUNK], F32, name="res", bufs=5)
+                nc.scalar.copy(out=res[:], in_=acc)
+                nc.sync.dma_start(out=out[:, chunks[0] * CHUNK : (chunks[0] + n) * CHUNK], in_=res[:])
 
         for chunks in ((0, 1), (2, 3), (4, 5), (6, 7)):
             finish(chunks)

from contextlib import ExitStack

import concourse.mybir as mybir
from concourse.masks import make_identity

K, T, S, N, H, U = 512, 2048, 512, 128, 512, 1024
FLOPS = 2 * K * H * S * 2 + 2 * H * N * U

F32 = mybir.dt.float32
BF16 = mybir.dt.bfloat16
I32 = mybir.dt.int32
U32 = mybir.dt.uint32
U16 = mybir.dt.uint16
U8 = mybir.dt.uint8
FP8X4 = mybir.dt.float8_e4m3fn_x4
FP4X4 = mybir.dt.float4_e2m1fn_x4
ACT = mybir.ActivationFunctionType
ALU = mybir.AluOpType

P = 128
PACK = 4
BLOCKS = H // P
CHUNK = 128
CHUNKS = U // CHUNK
SPAN = 256
SPANS = U // SPAN
BANKS = 8


def tile_picked_yttcpl_log_p_kernel(
    tc, x_words, x_scales, w1_words, w1_scales, w2_words, w2_scales, unit, w3_words, w3_scales, offs, me, ot, out
):
    nc = tc.nc
    with ExitStack() as ctx:
        keep = ctx.enter_context(tc.tile_pool(name="keep", bufs=1))
        ring = ctx.enter_context(tc.tile_pool(name="ring", bufs=2))
        psum = ctx.enter_context(tc.psum_pool(name="psum", bufs=1))

        offs_t = keep.tile([P, S // 16], U16, name="offs_t")
        me_t = keep.tile([P, U // 16], U16, name="me_t")
        ot_t = keep.tile([P, U // 16], U16, name="ot_t")
        xw = keep.tile([P, T], U32, name="xw", align_bytes=64)
        xs = keep.tile([P, T], U8, name="xs", align_bytes=64)
        w1w = keep.tile([P, 2 * H], U8, name="w1w", align_bytes=64)
        w2w = keep.tile([P, 2 * H], U8, name="w2w", align_bytes=64)
        w3w = keep.tile([P, 2 * N], U8, name="w3w", align_bytes=64)
        w1s = keep.tile([P, H], U8, name="w1s", align_bytes=64)
        w2s = keep.tile([P, H], U8, name="w2s", align_bytes=64)
        w3s = keep.tile([P, N], U8, name="w3s", align_bytes=64)
        unit_t = keep.tile([P, PACK], F32, name="unit_t")
        neg_unit = keep.tile([P, PACK], F32, name="neg_unit")
        ident = keep.tile([P, P], F32, name="ident")
        banks = [psum.tile([P, 512], F32, name="bank%d" % b) for b in range(BANKS)]

        def load_rows(queue, plane, rows, q):
            queue.dma_start(out=plane[32 * q : 32 * q + 4, :].bitcast(I32), in_=rows[0, 4 * q : 4 * q + 4, :].bitcast(I32))

        for plane in (xs, w2s, w1s, w3s):
            nc.vector.memset(plane[:].bitcast(I32), 0)
        nc.sync.dma_start(out=xw[:].bitcast(I32), in_=x_words[0].rearrange("p c r -> p (c r)").bitcast(I32))
        nc.sync.dma_start(offs_t[:], offs)
        for q in range(4):
            load_rows(nc.scalar, xs, x_scales, q)
        nc.sync.dma_start(out=w2w[:].bitcast(I32), in_=w2_words[0].bitcast(I32))
        for q in range(4):
            load_rows(nc.sync, w2s, w2_scales, q)
        nc.sync.dma_start(ot_t[:], ot)
        nc.sync.dma_start(me_t[:], me)
        nc.sync.dma_start(out=w1w[:].bitcast(I32), in_=w1_words[0].bitcast(I32))
        for q in range(4):
            load_rows(nc.sync, w1s, w1_scales, q)
        nc.sync.dma_start(out=unit_t[:], in_=unit.rearrange("(p t) o -> p (t o)", t=PACK))
        nc.sync.dma_start(out=w3w[:].bitcast(I32), in_=w3_words[0].bitcast(I32))
        for q in range(4):
            load_rows(nc.sync, w3s, w3_scales, q)
        warm = keep.tile([P, 2], F32, name="warm")
        nc.gpsimd.memset(warm[:, 0:1], 1.0)
        nc.scalar.activation(warm[:, 1:2], warm[:, 0:1], ACT.Ln)
        make_identity(nc, ident[:])

        xq_w = keep.tile([P, S], U32, name="xq_w", align_bytes=64)
        xq_s = keep.tile([P, S], U8, name="xq_s", align_bytes=64)
        nc.vector.tensor_copy(xq_s[:], xs[:].indirect(offs_t[:]))
        nc.vector.tensor_copy(xq_w[:], xw[:].indirect(offs_t[:]))

        def product(bank, words, plane, b):
            nc.tensor.matmul_mx(
                out=bank[:],
                lhsT=words[:, 2 * P * b : 2 * P * (b + 1)].bitcast(FP4X4),
                lhsT_scale=plane[:, P * b : P * (b + 1)],
                rhs=xq_w[:].bitcast(FP8X4),
                rhs_scale=xq_s[:],
                start=True,
                stop=True,
            )

        def turn(bank, t, source, start, stop):
            nc.tensor.matmul(bank[:, P * t : P * (t + 1)], source, ident[:], start=start, stop=stop, is_transpose=True)

        def dealt(bank):
            return bank[:].rearrange("r (m t) -> r t m", t=PACK)

        def by_tile(ap):
            return ap.rearrange("r (t m) -> r t m", t=PACK)

        def in_rows(ap, a):
            return ap.rearrange("r (a m) -> r a m", a=a)

        GV, GS = (512, 256), 512
        d04 = keep.tile([P, CHUNKS * H], F32, name="d04")
        pos = keep.tile([P, BLOCKS, max(GV)], F32, name="pos")
        neg = keep.tile([P, 2, BLOCKS, U], F32, name="neg")
        rec = keep.tile([P, SPANS, 2 * H], F32, name="rec")
        logs = neg[:, 0]
        log_den = logs.rearrange("r b (k s m) -> r s b k m", k=SPANS, s=SPANS)
        num = keep.tile([P, SPANS, 2 * H], F32, name="num")
        ttc = [neg[:, 1, :, SPAN * ((s + 2) % SPANS) : SPAN * ((s + 2) % SPANS + 1)] for s in range(SPANS)]

        def differences(side, g, tables, plus, minus):
            for b in range(BLOCKS):
                r0, w = g * GV[side], GV[side]
                nc.vector.tensor_copy(pos[:, b, :w], tables[b][:].indirect(plus[:, r0 // 16 : (r0 + w) // 16]))
                if r0 % GS == 0:
                    nc.scalar.activation(
                        neg[:, side, b, r0 : r0 + GS], tables[b][:].indirect(minus[:, r0 // 16 : (r0 + GS) // 16]), ACT.Copy, scale=-1.0
                    )
                for r in range(r0, r0 + w, CHUNK):
                    bank = banks[(r // CHUNK) % 4]
                    turn(bank, b, pos[:, b, r - r0 : r - r0 + CHUNK], True, False)
                    turn(bank, b, neg[:, side, b, r : r + CHUNK], False, True)

        vx, px = [], []
        for b in range(BLOCKS):
            product(banks[b], w2w, w2s, b)
            table = keep.tile([P, S + 16], F32, name="vx%d" % b)
            nc.gpsimd.memset(table[:, S:], 0.0)
            if b % 2 == 0:
                nc.scalar.copy(out=table[:, :S], in_=banks[b][:])
            else:
                nc.vector.tensor_copy(out=table[:, :S], in_=banks[b][:])
            vx.append(table)
        for b in range(BLOCKS):
            product(banks[4 + b], w1w, w1s, b)
            table = keep.tile([P, S + 16], F32, name="px%d" % b)
            nc.gpsimd.memset(table[:, S:], 0.0)
            if b < 3:
                nc.scalar.copy(out=table[:, :S], in_=banks[4 + b][:])
            else:
                nc.vector.tensor_copy(out=table[:, :S], in_=banks[4 + b][:])
            px.append(table)
        nc.gpsimd.tensor_scalar(out=neg_unit[:], in0=unit_t[:], scalar1=-1.0, scalar2=0.0, op0=ALU.mult, op1=ALU.add)

        for g in range(U // GV[0]):
            differences(0, g, vx, me_t, ot_t)
            for s in range(g * GV[0] // SPAN, (g + 1) * GV[0] // SPAN):
                for c in (2 * s, 2 * s + 1):
                    nc.vector.tensor_scalar(out=by_tile(d04[:, H * c : H * (c + 1)]), in0=dealt(banks[c % 4]), scalar1=0.4, scalar2=None, op0=ALU.mult)
                    half = in_rows(d04[:, H * c : H * (c + 1)], 2)
                    nc.gpsimd.tensor_tensor(out=rec[:, 2 * (c % 2) : 2 * (c % 2) + 2, 256 * s : 256 * (s + 1)], in0=half, in1=half, op=ALU.mult)
        for s in range(SPANS):
            nc.scalar.activation(log_den[:, s], rec[:, :, 256 * s : 256 * (s + 1)].rearrange("r b (k m) -> r b k m", k=SPANS), ACT.Ln, bias=0.3, scale=6.25)
        total = [banks[(c + 4) % BANKS] for c in range(CHUNKS)]

        def add_term(c, term, start, stop):
            for t in range(PACK):
                turn(total[c], t, term[:, P * t : P * (t + 1)], start and t == 0, stop and t == PACK - 1)

        def closing(s):
            differences(1, s, px, ot_t, me_t)
            cls = ring.tile([P, 2 * H], F32, name="cls")
            for c in (2 * s, 2 * s + 1):
                nc.vector.scalar_tensor_tensor(
                    out=by_tile(cls[:, H * (c % 2) : H * (c % 2 + 1)]), in0=dealt(banks[c % 4]), scalar=2.5,
                    in1=by_tile(d04[:, H * c : H * (c + 1)]), op0=ALU.mult, op1=ALU.mult,
                )
            nc.vector.tensor_scalar(out=num[:, s, :], in0=cls[:], scalar1=0.0, scalar2=0.1, op0=ALU.max, op1=ALU.add)
            add_term(s, d04[:, H * s : H * (s + 1)], True, False)

        def time_to_collision(s):
            nc.vector.tensor_tensor(out=ttc[s], in0=in_rows(num[:, s, :], 4), in1=in_rows(rec[:, s, :], 4), op=ALU.mult)
            for c in (2 * s, 2 * s + 1):
                if c >= CHUNKS // 2:
                    add_term(c, d04[:, H * c : H * (c + 1)], True, False)
                for t in range(PACK):
                    turn(total[c], t, ttc[s][:, 2 * (c % 2) + t // 2, P * (t % 2) : P * (t % 2 + 1)], False, False)

        for s in range(SPANS - 1):
            closing(s)
        for s in range(SPANS):
            nc.scalar.activation(rec[:, s, :].rearrange("r (b k m) -> r b k m", b=BLOCKS, k=SPANS), log_den[:, s], ACT.Exp, scale=-1.0)
        time_to_collision(0)
        closing(SPANS - 1)
        for s in range(1, SPANS):
            time_to_collision(s)

        def finish(chunks):
            s, n = chunks[0] // 2, len(chunks)
            cols = slice(H * (chunks[0] % 2), H * (chunks[0] % 2 + n))
            nc.scalar.activation(in_rows(rec[:, s, :], 4), ttc[s], ACT.Square)
            nc.scalar.activation(logs[:, s, cols], rec[:, s, cols], ACT.Ln, bias=0.3)
            for chunks in ([chunks] if s < SPANS - 1 else [(c,) for c in chunks]):
                n = len(chunks)
                hid = ring.tile([P, n * H], BF16, name="hid", align_bytes=64)
                for k, c in enumerate(chunks):
                    add_term(c, logs[:, s, H * (c % 2) : H * (c % 2 + 1)], False, True)
                    nc.vector.tensor_tensor(
                        out=hid[:, k * H : (k + 1) * H].rearrange("p (r t) -> p r t", t=PACK),
                        in0=total[c][:].rearrange("p (t r) -> p r t", t=PACK),
                        in1=neg_unit[:].unsqueeze(1).to_broadcast([P, CHUNK, PACK]),
                        op=ALU.mult,
                    )
                codes = ring.tile([P, n * CHUNK], U32, name="codes", align_bytes=64)
                scales = ring.tile([P, n * CHUNK], U8, name="scales", align_bytes=64)
                nc.vector.quantize_mx(out=codes[:].bitcast(FP8X4), scales=scales[:], in_=hid[:])
                acc = total[chunks[0]][:, 0 : n * CHUNK]
                nc.tensor.matmul_mx(
                    out=acc, lhsT=w3w[:].bitcast(FP4X4), lhsT_scale=w3s[:], rhs=codes[:].bitcast(FP8X4), rhs_scale=scales[:],
                    start=True, stop=True,
                )
                res = ring.tile([P, n * CHUNK], F32, name="res", bufs=5)
                nc.scalar.copy(out=res[:], in_=acc)
                nc.sync.dma_start(out=out[:, chunks[0] * CHUNK : (chunks[0] + n) * CHUNK], in_=res[:])

        for chunks in ((0, 1), (2, 3), (4, 5), (6, 7)):
            finish(chunks)
